import numpy as np
import ml_dtypes


def mxq(x, axis, fmt="e4m3"):
    dtype, down = {"e4m3": (ml_dtypes.float8_e4m3fn, 7), "e5m2": (ml_dtypes.float8_e5m2, 14)}[fmt]
    v = np.moveaxis(np.asarray(x, np.float32).astype(ml_dtypes.bfloat16).astype(np.float64), axis, -1)
    blocks = v.reshape(v.shape[:-1] + (-1, 32))
    amax = np.abs(blocks).max(-1, keepdims=True)
    byte = np.maximum(np.where(amax > 0, np.frexp(amax)[1] - 1 + 127, 0) - down, 1)
    scale = np.exp2(byte - 127.0)
    codes = (blocks / scale).astype(np.float32).astype(dtype).astype(np.float64)
    return np.moveaxis((codes * scale).reshape(v.shape), -1, axis)


WIDE = False


def mx_kscale(k):
    if not WIDE:
        return np.ones(k)
    levels = np.array([10, -10, 5, -5, 0])
    if k % 512:
        return np.exp2(np.random.permutation(np.resize(levels, k // 32))).repeat(32)
    a = np.empty((k // 512, 16))
    for p in range(k // 512):
        a[p, :8] = np.random.permutation(np.resize(levels, 8))
        for g in range(8):
            far = levels[np.abs(levels - a[p, g]) >= 10]
            a[p, g + 8] = far[np.random.randint(len(far))]
    return np.exp2(a.ravel()).repeat(32)


def f64(x):
    return np.asarray(x).astype(np.float64)


def striped8(idx):
    return np.concatenate([v.reshape(-1, 16).T for v in idx]).astype(np.uint16)


def unstriped8(offs):
    return np.stack([offs[16 * g:16 * g + 16].T.reshape(-1) for g in range(8)]).astype(np.int64)


E2M1 = np.array([0.0, 0.5, 1.0, 1.5, 2.0, 3.0, 4.0, 6.0, -0.0, -0.5, -1.0, -1.5, -2.0, -3.0, -4.0, -6.0])


def pack_weight(w, fmt):
    k, n = w.shape
    w = f64(np.asarray(w, np.float32).astype(ml_dtypes.bfloat16)).reshape(k // 32, 32, n)
    amax = np.abs(w).max(1)
    if fmt == "e4m3":
        byte = np.frexp(amax)[1] - 1 + 127 - 7
    else:
        mant, ex = np.frexp(amax / 6.0)
        byte = np.where(mant > 0.5, ex, ex - 1) + 127
    byte = np.clip(np.where(amax > 0, byte, 1), 1, 254)
    scaled = (w * np.exp2(127.0 - byte)[:, None, :]).reshape(k, n).astype(np.float32)
    by_word = np.ascontiguousarray(scaled.reshape(k // 512, 128, 4, n).transpose(0, 1, 3, 2))
    if fmt == "e4m3":
        words = by_word.astype(ml_dtypes.float8_e4m3fn).view(np.uint8)
    else:
        c = by_word.astype(ml_dtypes.float4_e2m1fn).view(np.uint8) & 0xF
        words = (c[..., 0::2] | (c[..., 1::2] << 4)).reshape(k // 512, 128, 2 * n)
    return np.ascontiguousarray(words), np.ascontiguousarray(byte.astype(np.uint8).reshape(k // 512, 16, n))


def unpack_weight(words, scales, fmt):
    g, _, n = scales.shape
    words = np.ascontiguousarray(words).reshape(g, 128, n, -1)
    if fmt == "e4m3":
        vals = words.view(ml_dtypes.float8_e4m3fn).astype(np.float64)
    else:
        nib = np.empty((g, 128, n, 4), np.uint8)
        nib[..., 0::2] = words & 0xF
        nib[..., 1::2] = words >> 4
        vals = E2M1[nib]
    vals = vals * np.repeat(np.exp2(scales.astype(np.float64) - 127.0), 8, axis=1)[..., None]
    return vals.transpose(0, 1, 3, 2).reshape(g * 512, n)


K, R, M, T, S = 1536, 512, 1024, 1024, 512


def setup_inputs():
    n = np.random.standard_normal
    s = mx_kscale(K)[:, None]
    u = mx_kscale(R)[:, None]
    p_w4 = pack_weight(n((K, M)) / np.sqrt(K) / s, "e2m1")
    return {
        "xT": (n((K, T)) * s).astype(np.float32),
        "w4_words": p_w4[0],
        "w4_scales": p_w4[1],
        "down": (n((K, R)) / np.sqrt(K) / s * u.T).astype(np.float32),
        "up": (0.5 * n((R, M)) / np.sqrt(R) / u).astype(np.float32),
        "wgt": np.repeat(np.random.uniform(0.5, 2.0, (8, S)), 16, axis=0).astype(np.float32),
        "offs": striped8(np.stack([np.random.permutation(T)[:S] for _ in range(8)])),
    }


def reference(xT, w4_words, w4_scales, down, up, wgt, offs):
    idx = unstriped8(offs)
    group = np.arange(K) % 512 // 64
    xg = f64(wgt)[np.arange(K) // 4 % 128] * f64(xT)[np.arange(K)[:, None], idx[group]]
    xT_ = mxq(xg, 0, "e4m3")
    w4_ = unpack_weight(w4_words, w4_scales, "e2m1")
    down_ = mxq(f64(down), 0, "e4m3")
    up_ = mxq(f64(up), 0, "e4m3")
    h_ = mxq(down_.T @ xT_, 0, "e4m3")
    y = w4_.T @ xT_ + up_.T @ h_
    return y

@@ -1,0 +1,303 @@
+from contextlib import ExitStack
+
+import concourse.mybir as mybir
+
+K, R, M, T, S = 1536, 512, 1024, 1024, 512
+FLOPS = 2 * S * (K * R + K * M + R * M)
+
+F32 = mybir.dt.float32
+BF16 = mybir.dt.bfloat16
+U32 = mybir.dt.uint32
+I32 = mybir.dt.int32
+U16 = mybir.dt.uint16
+U8 = mybir.dt.uint8
+E4M3 = mybir.dt.float8_e4m3fn_x4
+E2M1 = mybir.dt.float4_e2m1fn_x4
+MULT = mybir.AluOpType.mult
+
+P = 128
+PASSES = K // 512
+HALF = S // 2
+EARLY = 4
+
+
+def tile_list_hlora_none_kernel(tc, xT, w4_words, w4_scales, down, up, wgt, offs, out):
+    nc = tc.nc
+    with ExitStack() as ctx:
+        keep = ctx.enter_context(tc.tile_pool(name="keep", bufs=1))
+        psum = ctx.enter_context(tc.psum_pool(name="psum", bufs=1))
+
+        offsets = keep.tile([P, S // 16], U16, name="offsets")
+        weights = keep.tile([P, S], F32, name="weights")
+        x = [[keep.tile([P, T], F32, name=f"x{a}{t}") for t in range(4)] for a in range(PASSES)]
+        picked = [keep.tile([P, 4, S], F32, name=f"picked{a}") for a in range(PASSES)]
+        x_grouped = [keep.tile([P, S, 4], BF16, name=f"xgrouped{a}", align_bytes=64) for a in range(PASSES)]
+        x_codes = keep.tile([P, PASSES, S], U32, name="xcodes", align_bytes=64)
+        x_scales = keep.tile([P, PASSES, S], U8, name="xscales", align_bytes=64)
+        d_raw = [keep.tile([P, 4, R], F32, name=f"draw{a}") for a in range(PASSES)]
+        d_grouped = [keep.tile([P, R * 4], BF16, name=f"dgrouped{a}", align_bytes=64) for a in range(PASSES)]
+        d_codes = keep.tile([P, PASSES, R], U32, name="dcodes", align_bytes=64)
+        d_scales = keep.tile([P, PASSES, R], U8, name="dscales", align_bytes=64)
+        u_raw = [keep.tile([P, 4, M // 2], F32, name=f"uraw{a}") for a in range(2)]
+        u_grouped = [keep.tile([P, M // 2, 4], BF16, name=f"ugrouped{a}", align_bytes=64) for a in range(2)]
+        u_codes = keep.tile([P, M], U32, name="ucodes", align_bytes=64)
+        u_scales = keep.tile([P, M], U8, name="uscales", align_bytes=64)
+        w_codes = keep.tile([P, PASSES, 2 * M], U8, name="wcodes", align_bytes=64)
+        w_scales = keep.tile([P, PASSES, M], U8, name="wscales", align_bytes=64)
+        h_flat = keep.tile([P, 4, S], BF16, name="hflat", align_bytes=64)
+        h_grouped = keep.tile([P, S, 4], BF16, name="hgrouped", align_bytes=64)
+        h_codes = keep.tile([P, S], U32, name="hcodes", align_bytes=64)
+        h_scales = keep.tile([P, S], U8, name="hscales", align_bytes=64)
+        staged = [keep.tile([P, S], F32, name=f"staged{n}") for n in range(8)]
+
+        nc.sync.dma_start(offsets[:], offs)
+        nc.sync.dma_start(weights[:], wgt)
+        nc.vector.memset(w_scales[:].bitcast(I32), 0)
+        for q in range(4):
+            nc.scalar.dma_start(
+                out=w_scales[32 * q : 32 * q + 4].bitcast(I32),
+                in_=w4_scales[:, 4 * q : 4 * q + 4, :].bitcast(I32).rearrange("a q c -> q a c"),
+            )
+
+        def load_x(a, t):
+            nc.sync.dma_start(out=x[a][t][:], in_=xT[512 * a : 512 * a + 512, :].rearrange("(p t) c -> p t c", t=4)[:, t, :])
+
+        def load_d(a):
+            nc.sync.dma_start(out=d_raw[a][:], in_=down[512 * a : 512 * a + 512, :].rearrange("(p t) r -> p t r", t=4))
+
+        def load_w(n0, n1):
+            nc.sync.dma_start(
+                out=w_codes[:].bitcast(I32)[:, :, 64 * n0 : 64 * n1],
+                in_=w4_words.bitcast(I32).rearrange("a p c -> p a c")[:, :, 64 * n0 : 64 * n1],
+            )
+
+        def load_u(h):
+            nc.sync.dma_start(out=u_raw[h][:], in_=up.rearrange("(p t) n -> p t n", t=4)[:, :, 512 * h : 512 * h + 512])
+
+        for t in range(4):
+            load_x(0, t)
+        for t in range(3):
+            load_x(1, t)
+        load_d(0)
+        load_x(1, 3)
+        load_x(2, 0)
+        load_x(2, 1)
+        load_d(1)
+        load_x(2, 2)
+        load_x(2, 3)
+        load_w(0, EARLY)
+        load_d(2)
+        load_u(0)
+        load_w(EARLY, 8)
+        load_u(1)
+
+        def gather(a, t, h):
+            cols = slice(h * HALF, (h + 1) * HALF)
+            nc.vector.tensor_tensor(
+                picked[a][:, t, cols],
+                x[a][t][:].indirect(offsets[:, h * HALF // 16 : (h + 1) * HALF // 16]),
+                weights[:, cols],
+                MULT,
+            )
+
+        def copy_on(engine):
+            return nc.scalar.copy if engine == "S" else nc.vector.tensor_copy
+
+        def group_x(a, c0, c1, engine):
+            copy_on(engine)(
+                out=x_grouped[a][:, c0:c1, :].rearrange("p (c i) t -> p c t i", i=4),
+                in_=picked[a][:, :, c0:c1].rearrange("p t (c i) -> p c t i", i=4),
+            )
+
+        def quantize_x(a, h):
+            cols = slice(h * HALF, (h + 1) * HALF)
+            nc.vector.quantize_mx(
+                out=x_codes[:, a, cols].bitcast(E4M3), scales=x_scales[:, a, cols], in_=x_grouped[a][:, cols, :].rearrange("p c t -> p (c t)")
+            )
+
+        def group_d(a, m0, m1, engine):
+            copy_on(engine)(
+                out=d_grouped[a][:].rearrange("p (t m j) -> p m t j", t=4, j=4)[:, m0:m1],
+                in_=d_raw[a][:].rearrange("p j (m t) -> p m t j", t=4)[:, m0:m1],
+            )
+
+        def quantize_d(a):
+            nc.vector.quantize_mx(out=d_codes[:, a, :].bitcast(E4M3), scales=d_scales[:, a, :], in_=d_grouped[a][:])
+
+        def group_u(h, c0, c1, engine):
+            copy_on(engine)(
+                out=u_grouped[h][:, c0:c1, :].rearrange("p (c i) t -> p c t i", i=4),
+                in_=u_raw[h][:, :, c0:c1].rearrange("p t (c i) -> p c t i", i=4),
+            )
+
+        def quantize_u(h):
+            cols = slice(512 * h, 512 * h + 512)
+            nc.vector.quantize_mx(
+                out=u_codes[:, cols].bitcast(E4M3), scales=u_scales[:, cols], in_=u_grouped[h][:].rearrange("p c t -> p (c t)")
+            )
+
+        acc = {}
+
+        def base(n, a):
+            if a == 0:
+                acc[n] = psum.tile([P, S], F32, name=f"acc{n}" if n < EARLY else f"bank{n - 4}")
+            nc.tensor.matmul_mx(
+                out=acc[n][:],
+                lhsT=w_codes[:, a, 256 * n : 256 * n + 256].bitcast(E2M1),
+                lhsT_scale=w_scales[:, a, 128 * n : 128 * n + 128],
+                rhs=x_codes[:, a, :].bitcast(E4M3),
+                rhs_scale=x_scales[:, a, :],
+                start=(a == 0),
+                stop=False,
+            )
+
+        h_bank = {}
+
+        def low_rank(t, a):
+            if a == 0:
+                h_bank[t] = psum.tile([P, S], F32, name=f"bank{t}")
+            nc.tensor.matmul_mx(
+                out=h_bank[t][:],
+                lhsT=d_codes[:, a, 128 * t : 128 * t + 128].bitcast(E4M3),
+                lhsT_scale=d_scales[:, a, 128 * t : 128 * t + 128],
+                rhs=x_codes[:, a, :].bitcast(E4M3),
+                rhs_scale=x_scales[:, a, :],
+                start=(a == 0),
+                stop=(a == PASSES - 1),
+            )
+
+        def empty_h(t, engine):
+            copy_on(engine)(out=h_flat[:, t, :], in_=h_bank[t][:])
+
+        def group_h(c0, c1, engine):
+            copy_on(engine)(
+                out=h_grouped[:, c0:c1, :].rearrange("p (c i) t -> p c t i", i=4),
+                in_=h_flat[:, :, c0:c1].rearrange("p t (c i) -> p c t i", i=4),
+            )
+
+        def quantize_h():
+            nc.vector.quantize_mx(out=h_codes[:].bitcast(E4M3), scales=h_scales[:], in_=h_grouped[:].rearrange("p c t -> p (c t)"))
+
+        def finish(n):
+            nc.tensor.matmul_mx(
+                out=acc[n][:],
+                lhsT=u_codes[:, 128 * n : 128 * n + 128].bitcast(E4M3),
+                lhsT_scale=u_scales[:, 128 * n : 128 * n + 128],
+                rhs=h_codes[:].bitcast(E4M3),
+                rhs_scale=h_scales[:],
+                start=False,
+                stop=True,
+            )
+
+        def empty_out(n, engine):
+            copy_on(engine)(out=staged[n][:], in_=acc[n][:])
+            nc.sync.dma_start(out=out[128 * n : 128 * n + 128, :], in_=staged[n][:])
+
+        gather(0, 0, 0)
+        gather(0, 0, 1)
+        gather(0, 1, 0)
+        gather(0, 1, 1)
+        gather(0, 2, 0)
+        gather(0, 2, 1)
+        gather(0, 3, 0)
+        gather(0, 3, 1)
+        group_x(0, 0, HALF, "S")
+        group_x(0, HALF, S, "S")
+        gather(1, 0, 0)
+        gather(1, 0, 1)
+        gather(1, 1, 0)
+        quantize_x(0, 0)
+        gather(1, 1, 1)
+        gather(1, 2, 0)
+        gather(1, 2, 1)
+        quantize_x(0, 1)
+        group_d(0, 0, 128, "S")
+        gather(1, 3, 0)
+        gather(1, 3, 1)
+        group_x(1, 0, HALF, "S")
+        group_x(1, HALF, S, "S")
+        gather(2, 0, 0)
+        gather(2, 0, 1)
+        gather(2, 1, 0)
+        quantize_x(1, 0)
+        gather(2, 1, 1)
+        quantize_d(0)
+        quantize_x(1, 1)
+        group_d(1, 0, 128, "S")
+        low_rank(0, 0)
+        low_rank(1, 0)
+        low_rank(2, 0)
+        low_rank(3, 0)
+        base(0, 0)
+        base(1, 0)
+        base(2, 0)
+        base(3, 0)
+        base(0, 1)
+        base(1, 1)
+        base(2, 1)
+        base(3, 1)
+        gather(2, 2, 0)
+        gather(2, 2, 1)
+        gather(2, 3, 0)
+        group_x(2, 0, HALF, "S")
+        gather(2, 3, 1)
+        quantize_d(1)
+        low_rank(0, 1)
+        low_rank(1, 1)
+        low_rank(2, 1)
+        low_rank(3, 1)
+        group_x(2, HALF, S, "V")
+        quantize_x(2, 0)
+        group_d(2, 0, 64, "S")
+        group_d(2, 64, 128, "V")
+        quantize_x(2, 1)
+        quantize_d(2)
+        low_rank(0, 2)
+        low_rank(1, 2)
+        low_rank(2, 2)
+        low_rank(3, 2)
+        base(0, 2)
+        base(1, 2)
+        base(2, 2)
+        base(3, 2)
+        empty_h(0, "S")
+        empty_h(1, "V")
+        group_u(0, 0, 256, "S")
+        empty_h(2, "S")
+        empty_h(3, "V")
+        group_u(0, 256, 512, "V")
+        group_h(0, 64, "S")
+        group_h(64, 512, "V")
+        quantize_h()
+        quantize_u(0)
+        base(4, 0)
+        base(4, 1)
+        base(4, 2)
+        base(5, 0)
+        base(5, 1)
+        base(5, 2)
+        base(6, 0)
+        base(6, 1)
+        base(6, 2)
+        base(7, 0)
+        base(7, 1)
+        base(7, 2)
+        finish(0)
+        finish(1)
+        finish(2)
+        finish(3)
+        group_u(1, 0, 448, "S")
+        empty_out(0, "S")
+        empty_out(1, "V")
+        group_u(1, 448, 512, "V")
+        quantize_u(1)
+        empty_out(2, "S")
+        empty_out(3, "V")
+        finish(4)
+        finish(5)
+        finish(6)
+        finish(7)
+        empty_out(4, "S")
+        empty_out(5, "V")
+        empty_out(6, "S")
+        empty_out(7, "V")

@@ -19,6 +19,7 @@ P = 128
 PASSES = K // 512
 HALF = S // 2
 EARLY = 4
+U_COLS = 256
 
 
 def tile_list_hlora_none_kernel(tc, xT, w4_words, w4_scales, down, up, wgt, offs, out):
@@ -38,8 +39,8 @@ def tile_list_hlora_none_kernel(tc, xT, w4_words, w4_scales, down, up, wgt, offs
         d_grouped = [keep.tile([P, R * 4], BF16, name=f"dgrouped{a}", align_bytes=64) for a in range(PASSES)]
         d_codes = keep.tile([P, PASSES, R], U32, name="dcodes", align_bytes=64)
         d_scales = keep.tile([P, PASSES, R], U8, name="dscales", align_bytes=64)
-        u_raw = [keep.tile([P, 4, M // 2], F32, name=f"uraw{a}") for a in range(2)]
-        u_grouped = [keep.tile([P, M // 2, 4], BF16, name=f"ugrouped{a}", align_bytes=64) for a in range(2)]
+        u_raw = [keep.tile([P, 4, U_COLS], F32, name=f"uraw{c}") for c in range(M // U_COLS)]
+        u_grouped = {c: keep.tile([P, U_COLS, 4], BF16, name=f"ugrouped{c}", align_bytes=64) for c in [1]}
         u_codes = keep.tile([P, M], U32, name="ucodes", align_bytes=64)
         u_scales = keep.tile([P, M], U8, name="uscales", align_bytes=64)
         w_codes = keep.tile([P, PASSES, 2 * M], U8, name="wcodes", align_bytes=64)
@@ -65,31 +66,38 @@ def tile_list_hlora_none_kernel(tc, xT, w4_words, w4_scales, down, up, wgt, offs
         def load_d(a):
             nc.sync.dma_start(out=d_raw[a][:], in_=down[512 * a : 512 * a + 512, :].rearrange("(p t) r -> p t r", t=4))
 
-        def load_w(n0, n1):
+        def load_w(a0, a1, n0, n1):
             nc.sync.dma_start(
-                out=w_codes[:].bitcast(I32)[:, :, 64 * n0 : 64 * n1],
-                in_=w4_words.bitcast(I32).rearrange("a p c -> p a c")[:, :, 64 * n0 : 64 * n1],
+                out=w_codes[:].bitcast(I32)[:, a0:a1, 64 * n0 : 64 * n1],
+                in_=w4_words.bitcast(I32).rearrange("a p c -> p a c")[:, a0:a1, 64 * n0 : 64 * n1],
             )
 
-        def load_u(h):
-            nc.sync.dma_start(out=u_raw[h][:], in_=up.rearrange("(p t) n -> p t n", t=4)[:, :, 512 * h : 512 * h + 512])
+        def load_u(c):
+            nc.sync.dma_start(out=u_raw[c][:], in_=up.rearrange("(p t) n -> p t n", t=4)[:, :, U_COLS * c : U_COLS * c + U_COLS])
 
-        for t in range(4):
-            load_x(0, t)
-        for t in range(3):
-            load_x(1, t)
-        load_d(0)
+        load_x(0, 0)
+        load_x(0, 1)
+        load_x(0, 2)
+        load_x(0, 3)
+        load_x(1, 0)
+        load_x(1, 1)
+        load_x(1, 2)
         load_x(1, 3)
         load_x(2, 0)
         load_x(2, 1)
-        load_d(1)
+        load_d(0)
         load_x(2, 2)
+        load_d(1)
         load_x(2, 3)
-        load_w(0, EARLY)
+        load_w(0, 1, 0, EARLY)
         load_d(2)
+        load_w(1, 2, 0, EARLY)
         load_u(0)
-        load_w(EARLY, 8)
+        load_w(0, 3, EARLY, 8)
         load_u(1)
+        load_u(2)
+        load_w(2, 3, 0, EARLY)
+        load_u(3)
 
         def gather(a, t, h):
             cols = slice(h * HALF, (h + 1) * HALF)
@@ -109,10 +117,9 @@ def tile_list_hlora_none_kernel(tc, xT, w4_words, w4_scales, down, up, wgt, offs
                 in_=picked[a][:, :, c0:c1].rearrange("p t (c i) -> p c t i", i=4),
             )
 
-        def quantize_x(a, h):
-            cols = slice(h * HALF, (h + 1) * HALF)
+        def quantize_x(a):
             nc.vector.quantize_mx(
-                out=x_codes[:, a, cols].bitcast(E4M3), scales=x_scales[:, a, cols], in_=x_grouped[a][:, cols, :].rearrange("p c t -> p (c t)")
+                out=x_codes[:, a, :].bitcast(E4M3), scales=x_scales[:, a, :], in_=x_grouped[a][:].rearrange("p c t -> p (c t)")
             )
 
         def group_d(a, m0, m1, engine):
@@ -124,16 +131,16 @@ def tile_list_hlora_none_kernel(tc, xT, w4_words, w4_scales, down, up, wgt, offs
         def quantize_d(a):
             nc.vector.quantize_mx(out=d_codes[:, a, :].bitcast(E4M3), scales=d_scales[:, a, :], in_=d_grouped[a][:])
 
-        def group_u(h, c0, c1, engine):
+        def group_u(c, c0, c1, engine):
             copy_on(engine)(
-                out=u_grouped[h][:, c0:c1, :].rearrange("p (c i) t -> p c t i", i=4),
-                in_=u_raw[h][:, :, c0:c1].rearrange("p t (c i) -> p c t i", i=4),
+                out=u_grouped[c][:, c0:c1, :].rearrange("p (c i) t -> p c t i", i=4),
+                in_=u_raw[c][:, :, c0:c1].rearrange("p t (c i) -> p c t i", i=4),
             )
 
-        def quantize_u(h):
-            cols = slice(512 * h, 512 * h + 512)
+        def quantize_u(c):
+            cols = slice(U_COLS * c, U_COLS * c + U_COLS)
             nc.vector.quantize_mx(
-                out=u_codes[:, cols].bitcast(E4M3), scales=u_scales[:, cols], in_=u_grouped[h][:].rearrange("p c t -> p (c t)")
+                out=u_codes[:, cols].bitcast(E4M3), scales=u_scales[:, cols], in_=u_grouped[c][:].rearrange("p c t -> p (c t)")
             )
 
         acc = {}
@@ -189,115 +196,133 @@ def tile_list_hlora_none_kernel(tc, xT, w4_words, w4_scales, down, up, wgt, offs
                 stop=True,
             )
 
-        def empty_out(n, engine):
-            copy_on(engine)(out=staged[n][:], in_=acc[n][:])
+        def empty_out(n, c0, c1, engine):
+            copy_on(engine)(out=staged[n][:, c0:c1], in_=acc[n][:, c0:c1])
+
+        def store(n):
             nc.sync.dma_start(out=out[128 * n : 128 * n + 128, :], in_=staged[n][:])
 
-        gather(0, 0, 0)
         gather(0, 0, 1)
+        gather(0, 0, 0)
         gather(0, 1, 0)
         gather(0, 1, 1)
-        gather(0, 2, 0)
         gather(0, 2, 1)
-        gather(0, 3, 0)
+        gather(0, 2, 0)
         gather(0, 3, 1)
-        group_x(0, 0, HALF, "S")
+        gather(0, 3, 0)
         group_x(0, HALF, S, "S")
         gather(1, 0, 0)
-        gather(1, 0, 1)
-        gather(1, 1, 0)
-        quantize_x(0, 0)
         gather(1, 1, 1)
+        group_x(0, 0, HALF, "S")
+        gather(1, 0, 1)
         gather(1, 2, 0)
-        gather(1, 2, 1)
-        quantize_x(0, 1)
-        group_d(0, 0, 128, "S")
-        gather(1, 3, 0)
+        gather(1, 1, 0)
         gather(1, 3, 1)
-        group_x(1, 0, HALF, "S")
-        group_x(1, HALF, S, "S")
+        gather(1, 3, 0)
         gather(2, 0, 0)
-        gather(2, 0, 1)
+        group_x(1, 0, HALF, "S")
+        quantize_x(0)
+        gather(1, 2, 1)
         gather(2, 1, 0)
-        quantize_x(1, 0)
+        group_x(1, HALF, S, "S")
         gather(2, 1, 1)
-        quantize_d(0)
-        quantize_x(1, 1)
-        group_d(1, 0, 128, "S")
-        low_rank(0, 0)
-        low_rank(1, 0)
-        low_rank(2, 0)
-        low_rank(3, 0)
-        base(0, 0)
-        base(1, 0)
-        base(2, 0)
-        base(3, 0)
-        base(0, 1)
-        base(1, 1)
-        base(2, 1)
-        base(3, 1)
-        gather(2, 2, 0)
+        gather(2, 0, 1)
+        group_d(0, 0, 128, "S")
+        quantize_x(1)
         gather(2, 2, 1)
+        gather(2, 2, 0)
+        quantize_d(0)
+        group_d(1, 0, 96, "S")
+        group_d(1, 96, 128, "V")
+        low_rank(3, 0)
+        low_rank(0, 0)
         gather(2, 3, 0)
-        group_x(2, 0, HALF, "S")
+        low_rank(1, 0)
+        base(3, 0)
         gather(2, 3, 1)
+        low_rank(2, 0)
+        group_x(2, 0, HALF, "S")
+        base(2, 0)
+        base(1, 0)
         quantize_d(1)
-        low_rank(0, 1)
-        low_rank(1, 1)
-        low_rank(2, 1)
-        low_rank(3, 1)
+        base(0, 0)
         group_x(2, HALF, S, "V")
-        quantize_x(2, 0)
+        low_rank(1, 1)
+        low_rank(3, 1)
         group_d(2, 0, 64, "S")
         group_d(2, 64, 128, "V")
-        quantize_x(2, 1)
+        low_rank(2, 1)
+        low_rank(0, 1)
+        quantize_x(2)
+        base(1, 1)
+        base(0, 1)
+        base(3, 1)
         quantize_d(2)
-        low_rank(0, 2)
-        low_rank(1, 2)
+        base(2, 1)
         low_rank(2, 2)
         low_rank(3, 2)
-        base(0, 2)
-        base(1, 2)
-        base(2, 2)
-        base(3, 2)
-        empty_h(0, "S")
+        empty_h(2, "V")
+        low_rank(1, 2)
+        empty_h(3, "S")
+        low_rank(0, 2)
         empty_h(1, "V")
-        group_u(0, 0, 256, "S")
-        empty_h(2, "S")
-        empty_h(3, "V")
-        group_u(0, 256, 512, "V")
-        group_h(0, 64, "S")
-        group_h(64, 512, "V")
-        quantize_h()
-        quantize_u(0)
-        base(4, 0)
-        base(4, 1)
-        base(4, 2)
-        base(5, 0)
-        base(5, 1)
-        base(5, 2)
         base(6, 0)
-        base(6, 1)
-        base(6, 2)
+        empty_h(0, "S")
         base(7, 0)
+        group_u(1, 64, 256, "V")
+        base(6, 1)
+        group_u(1, 0, 64, "S")
+        base(5, 0)
+        group_h(128, 512, "V")
+        base(6, 2)
+        group_h(0, 128, "S")
+        base(5, 1)
         base(7, 1)
-        base(7, 2)
-        finish(0)
-        finish(1)
-        finish(2)
-        finish(3)
-        group_u(1, 0, 448, "S")
-        empty_out(0, "S")
-        empty_out(1, "V")
-        group_u(1, 448, 512, "V")
+        base(5, 2)
         quantize_u(1)
-        empty_out(2, "S")
-        empty_out(3, "V")
-        finish(4)
+        base(7, 2)
+        held = keep.tile([P, 2, U_COLS, 4], BF16, name="hflat", align_bytes=64)
+        u_grouped[0] = held[:, 0]
+        u_grouped[2] = held[:, 1]
+        group_u(0, 0, 192, "S")
+        quantize_h()
+        base(0, 2)
+        base(3, 2)
+        group_u(0, 192, 256, "V")
+        base(2, 2)
+        group_u(2, 64, 256, "V")
+        group_u(2, 0, 64, "S")
+        finish(3)
+        finish(2)
+        quantize_u(0)
+        empty_out(3, 0, S, "S")
+        store(3)
+        base(1, 2)
+        quantize_u(2)
+        base(4, 0)
+        finish(0)
+        held = keep.tile([P, 1, U_COLS, 4], BF16, name="hgrouped", align_bytes=64)
+        u_grouped[3] = held[:, 0]
+        group_u(3, 0, 256, "V")
+        empty_out(2, 0, S, "S")
+        store(2)
+        finish(1)
         finish(5)
-        finish(6)
+        empty_out(1, 0, S, "V")
+        store(1)
+        base(4, 1)
+        empty_out(0, 0, S, "S")
+        store(0)
+        base(4, 2)
+        quantize_u(3)
+        empty_out(5, 0, S, "S")
+        store(5)
+        finish(4)
         finish(7)
-        empty_out(4, "S")
-        empty_out(5, "V")
-        empty_out(6, "S")
-        empty_out(7, "V")
+        empty_out(4, 0, S, "V")
+        store(4)
+        finish(6)
+        empty_out(7, 0, S, "S")
+        store(7)
+        empty_out(6, 0, S, "V")
+        store(6)

@@ -40,7 +40,7 @@ def tile_list_hlora_none_kernel(tc, xT, w4_words, w4_scales, down, up, wgt, offs
         d_codes = keep.tile([P, PASSES, R], U32, name="dcodes", align_bytes=64)
         d_scales = keep.tile([P, PASSES, R], U8, name="dscales", align_bytes=64)
         u_raw = [keep.tile([P, 4, U_COLS], F32, name=f"uraw{c}") for c in range(M // U_COLS)]
-        u_grouped = {c: keep.tile([P, U_COLS, 4], BF16, name=f"ugrouped{c}", align_bytes=64) for c in [1]}
+        u_grouped = {c: keep.tile([P, U_COLS, 4], BF16, name=f"ugrouped{c}", align_bytes=64) for c in [0,1]}
         u_codes = keep.tile([P, M], U32, name="ucodes", align_bytes=64)
         u_scales = keep.tile([P, M], U8, name="uscales", align_bytes=64)
         w_codes = keep.tile([P, PASSES, 2 * M], U8, name="wcodes", align_bytes=64)
@@ -52,10 +52,10 @@ def tile_list_hlora_none_kernel(tc, xT, w4_words, w4_scales, down, up, wgt, offs
         staged = [keep.tile([P, S], F32, name=f"staged{n}") for n in range(8)]
 
         nc.sync.dma_start(offsets[:], offs)
-        nc.sync.dma_start(weights[:], wgt)
-        nc.vector.memset(w_scales[:].bitcast(I32), 0)
+        nc.sync.dma_start(weights[:, 0:HALF], wgt[:, 0:HALF])
+        nc.gpsimd.memset(w_scales[:].bitcast(I32), 0)
         for q in range(4):
-            nc.scalar.dma_start(
+            nc.gpsimd.dma_start(
                 out=w_scales[32 * q : 32 * q + 4].bitcast(I32),
                 in_=w4_scales[:, 4 * q : 4 * q + 4, :].bitcast(I32).rearrange("a q c -> q a c"),
             )
@@ -76,6 +76,7 @@ def tile_list_hlora_none_kernel(tc, xT, w4_words, w4_scales, down, up, wgt, offs
             nc.sync.dma_start(out=u_raw[c][:], in_=up.rearrange("(p t) n -> p t n", t=4)[:, :, U_COLS * c : U_COLS * c + U_COLS])
 
         load_x(0, 0)
+        nc.sync.dma_start(weights[:, HALF:S], wgt[:, HALF:S])
         load_x(0, 1)
         load_x(0, 2)
         load_x(0, 3)
@@ -84,19 +85,19 @@ def tile_list_hlora_none_kernel(tc, xT, w4_words, w4_scales, down, up, wgt, offs
         load_x(1, 2)
         load_x(1, 3)
         load_x(2, 0)
-        load_x(2, 1)
         load_d(0)
+        load_x(2, 1)
         load_x(2, 2)
         load_d(1)
         load_x(2, 3)
-        load_w(0, 1, 0, EARLY)
         load_d(2)
-        load_w(1, 2, 0, EARLY)
+        load_w(0, 1, 0, EARLY)
         load_u(0)
+        load_w(1, 2, 0, EARLY)
         load_w(0, 3, EARLY, 8)
+        load_w(2, 3, 0, EARLY)
         load_u(1)
         load_u(2)
-        load_w(2, 3, 0, EARLY)
         load_u(3)
 
         def gather(a, t, h):
@@ -202,8 +203,8 @@ def tile_list_hlora_none_kernel(tc, xT, w4_words, w4_scales, down, up, wgt, offs
         def store(n):
             nc.sync.dma_start(out=out[128 * n : 128 * n + 128, :], in_=staged[n][:])
 
-        gather(0, 0, 1)
         gather(0, 0, 0)
+        gather(0, 0, 1)
         gather(0, 1, 0)
         gather(0, 1, 1)
         gather(0, 2, 1)
@@ -212,117 +213,116 @@ def tile_list_hlora_none_kernel(tc, xT, w4_words, w4_scales, down, up, wgt, offs
         gather(0, 3, 0)
         group_x(0, HALF, S, "S")
         gather(1, 0, 0)
-        gather(1, 1, 1)
-        group_x(0, 0, HALF, "S")
         gather(1, 0, 1)
-        gather(1, 2, 0)
+        group_x(0, 0, HALF, "S")
         gather(1, 1, 0)
-        gather(1, 3, 1)
-        gather(1, 3, 0)
-        gather(2, 0, 0)
-        group_x(1, 0, HALF, "S")
-        quantize_x(0)
+        gather(1, 2, 0)
         gather(1, 2, 1)
-        gather(2, 1, 0)
+        gather(1, 3, 1)
+        gather(1, 1, 1)
+        gather(2, 0, 0)
         group_x(1, HALF, S, "S")
-        gather(2, 1, 1)
         gather(2, 0, 1)
-        group_d(0, 0, 128, "S")
-        quantize_x(1)
-        gather(2, 2, 1)
+        quantize_x(0)
+        group_d(0, 0, 96, "S")
+        group_d(0, 96, 128, "V")
+        gather(1, 3, 0)
+        gather(2, 1, 0)
+        gather(2, 1, 1)
+        group_x(1, 0, HALF, "S")
         gather(2, 2, 0)
+        gather(2, 2, 1)
+        quantize_x(1)
         quantize_d(0)
         group_d(1, 0, 96, "S")
         group_d(1, 96, 128, "V")
-        low_rank(3, 0)
         low_rank(0, 0)
+        low_rank(2, 0)
         gather(2, 3, 0)
         low_rank(1, 0)
-        base(3, 0)
+        low_rank(3, 0)
         gather(2, 3, 1)
-        low_rank(2, 0)
         group_x(2, 0, HALF, "S")
-        base(2, 0)
-        base(1, 0)
         quantize_d(1)
-        base(0, 0)
         group_x(2, HALF, S, "V")
         low_rank(1, 1)
-        low_rank(3, 1)
         group_d(2, 0, 64, "S")
+        low_rank(3, 1)
         group_d(2, 64, 128, "V")
-        low_rank(2, 1)
         low_rank(0, 1)
+        low_rank(2, 1)
         quantize_x(2)
-        base(1, 1)
-        base(0, 1)
-        base(3, 1)
+        base(1, 0)
+        base(2, 0)
+        group_u(0, 0, 192, "S")
+        base(3, 0)
         quantize_d(2)
+        base(0, 0)
         base(2, 1)
-        low_rank(2, 2)
-        low_rank(3, 2)
-        empty_h(2, "V")
+        group_u(0, 192, 256, "V")
+        base(1, 1)
         low_rank(1, 2)
+        quantize_u(0)
+        low_rank(3, 2)
+        empty_h(1, "V")
+        low_rank(2, 2)
         empty_h(3, "S")
         low_rank(0, 2)
-        empty_h(1, "V")
-        base(6, 0)
+        base(3, 1)
+        empty_h(2, "V")
+        base(0, 1)
         empty_h(0, "S")
-        base(7, 0)
+        base(2, 2)
         group_u(1, 64, 256, "V")
-        base(6, 1)
+        base(7, 0)
+        base(6, 0)
         group_u(1, 0, 64, "S")
-        base(5, 0)
-        group_h(128, 512, "V")
-        base(6, 2)
-        group_h(0, 128, "S")
-        base(5, 1)
         base(7, 1)
-        base(5, 2)
-        quantize_u(1)
-        base(7, 2)
-        held = keep.tile([P, 2, U_COLS, 4], BF16, name="hflat", align_bytes=64)
-        u_grouped[0] = held[:, 0]
-        u_grouped[2] = held[:, 1]
-        group_u(0, 0, 192, "S")
-        quantize_h()
+        group_h(128, 512, "V")
+        group_h(0, 128, "S")
+        base(4, 0)
         base(0, 2)
         base(3, 2)
-        group_u(0, 192, 256, "V")
-        base(2, 2)
-        group_u(2, 64, 256, "V")
-        group_u(2, 0, 64, "S")
-        finish(3)
-        finish(2)
-        quantize_u(0)
-        empty_out(3, 0, S, "S")
-        store(3)
+        quantize_u(1)
         base(1, 2)
-        quantize_u(2)
-        base(4, 0)
-        finish(0)
-        held = keep.tile([P, 1, U_COLS, 4], BF16, name="hgrouped", align_bytes=64)
-        u_grouped[3] = held[:, 0]
+        held = keep.tile([P, 2, U_COLS, 4], BF16, name="hflat", align_bytes=64)
+        u_grouped[2] = held[:, 0]
+        u_grouped[3] = held[:, 1]
+        group_u(2, 0, 256, "S")
+        quantize_h()
+        base(5, 0)
+        base(6, 1)
+        base(5, 1)
         group_u(3, 0, 256, "V")
+        finish(0)
+        finish(1)
+        empty_out(0, HALF, S, "V")
+        empty_out(0, 0, HALF, "S")
+        store(0)
+        finish(3)
+        base(5, 2)
+        quantize_u(2)
+        empty_out(1, 0, S, "S")
+        store(1)
+        finish(2)
+        empty_out(3, 0, S, "V")
+        store(3)
+        base(6, 2)
+        finish(5)
         empty_out(2, 0, S, "S")
         store(2)
-        finish(1)
-        finish(5)
-        empty_out(1, 0, S, "V")
-        store(1)
-        base(4, 1)
-        empty_out(0, 0, S, "S")
-        store(0)
-        base(4, 2)
         quantize_u(3)
-        empty_out(5, 0, S, "S")
+        base(7, 2)
+        base(4, 1)
+        empty_out(5, 0, S, "V")
         store(5)
-        finish(4)
         finish(7)
+        finish(6)
+        empty_out(7, 0, S, "V")
+        store(7)
+        base(4, 2)
+        empty_out(6, 0, S, "S")
+        store(6)
+        finish(4)
         empty_out(4, 0, S, "V")
         store(4)
-        finish(6)
-        empty_out(7, 0, S, "S")
-        store(7)
-        empty_out(6, 0, S, "V")
-        store(6)

from contextlib import ExitStack

import concourse.mybir as mybir

K, R, M, T, S = 1536, 512, 1024, 1024, 512
FLOPS = 2 * S * (K * R + K * M + R * M)

F32 = mybir.dt.float32
BF16 = mybir.dt.bfloat16
U32 = mybir.dt.uint32
I32 = mybir.dt.int32
U16 = mybir.dt.uint16
U8 = mybir.dt.uint8
E4M3 = mybir.dt.float8_e4m3fn_x4
E2M1 = mybir.dt.float4_e2m1fn_x4
MULT = mybir.AluOpType.mult

P = 128
PASSES = K // 512
HALF = S // 2
EARLY = 4
U_COLS = 256


def tile_list_hlora_none_kernel(tc, xT, w4_words, w4_scales, down, up, wgt, offs, out):
    nc = tc.nc
    with ExitStack() as ctx:
        keep = ctx.enter_context(tc.tile_pool(name="keep", bufs=1))
        psum = ctx.enter_context(tc.psum_pool(name="psum", bufs=1))

        offsets = keep.tile([P, S // 16], U16, name="offsets")
        weights = keep.tile([P, S], F32, name="weights")
        x = [[keep.tile([P, T], F32, name=f"x{a}{t}") for t in range(4)] for a in range(PASSES)]
        picked = [keep.tile([P, 4, S], F32, name=f"picked{a}") for a in range(PASSES)]
        x_grouped = [keep.tile([P, S, 4], BF16, name=f"xgrouped{a}", align_bytes=64) for a in range(PASSES)]
        x_codes = keep.tile([P, PASSES, S], U32, name="xcodes", align_bytes=64)
        x_scales = keep.tile([P, PASSES, S], U8, name="xscales", align_bytes=64)
        d_raw = [keep.tile([P, 4, R], F32, name=f"draw{a}") for a in range(PASSES)]
        d_grouped = [keep.tile([P, R * 4], BF16, name=f"dgrouped{a}", align_bytes=64) for a in range(PASSES)]
        d_codes = keep.tile([P, PASSES, R], U32, name="dcodes", align_bytes=64)
        d_scales = keep.tile([P, PASSES, R], U8, name="dscales", align_bytes=64)
        u_raw = [keep.tile([P, 4, U_COLS], F32, name=f"uraw{c}") for c in range(M // U_COLS)]
        u_grouped = {c: keep.tile([P, U_COLS, 4], BF16, name=f"ugrouped{c}", align_bytes=64) for c in [0,1]}
        u_codes = keep.tile([P, M], U32, name="ucodes", align_bytes=64)
        u_scales = keep.tile([P, M], U8, name="uscales", align_bytes=64)
        w_codes = keep.tile([P, PASSES, 2 * M], U8, name="wcodes", align_bytes=64)
        w_scales = keep.tile([P, PASSES, M], U8, name="wscales", align_bytes=64)
        h_flat = keep.tile([P, 4, S], BF16, name="hflat", align_bytes=64)
        h_grouped = keep.tile([P, S, 4], BF16, name="hgrouped", align_bytes=64)
        h_codes = keep.tile([P, S], U32, name="hcodes", align_bytes=64)
        h_scales = keep.tile([P, S], U8, name="hscales", align_bytes=64)
        staged = [keep.tile([P, S], F32, name=f"staged{n}") for n in range(8)]

        nc.sync.dma_start(offsets[:], offs)
        nc.sync.dma_start(weights[:, 0:HALF], wgt[:, 0:HALF])
        nc.gpsimd.memset(w_scales[:].bitcast(I32), 0)
        for q in range(4):
            nc.gpsimd.dma_start(
                out=w_scales[32 * q : 32 * q + 4].bitcast(I32),
                in_=w4_scales[:, 4 * q : 4 * q + 4, :].bitcast(I32).rearrange("a q c -> q a c"),
            )

        def load_x(a, t):
            nc.sync.dma_start(out=x[a][t][:], in_=xT[512 * a : 512 * a + 512, :].rearrange("(p t) c -> p t c", t=4)[:, t, :])

        def load_d(a):
            nc.sync.dma_start(out=d_raw[a][:], in_=down[512 * a : 512 * a + 512, :].rearrange("(p t) r -> p t r", t=4))

        def load_w(a0, a1, n0, n1):
            nc.sync.dma_start(
                out=w_codes[:].bitcast(I32)[:, a0:a1, 64 * n0 : 64 * n1],
                in_=w4_words.bitcast(I32).rearrange("a p c -> p a c")[:, a0:a1, 64 * n0 : 64 * n1],
            )

        def load_u(c):
            nc.sync.dma_start(out=u_raw[c][:], in_=up.rearrange("(p t) n -> p t n", t=4)[:, :, U_COLS * c : U_COLS * c + U_COLS])

        load_x(0, 0)
        nc.sync.dma_start(weights[:, HALF:S], wgt[:, HALF:S])
        load_x(0, 1)
        load_x(0, 2)
        load_x(0, 3)
        load_x(1, 0)
        load_x(1, 1)
        load_x(1, 2)
        load_x(1, 3)
        load_x(2, 0)
        load_d(0)
        load_x(2, 1)
        load_x(2, 2)
        load_d(1)
        load_x(2, 3)
        load_d(2)
        load_w(0, 1, 0, EARLY)
        load_u(0)
        load_w(1, 2, 0, EARLY)
        load_w(0, 3, EARLY, 8)
        load_w(2, 3, 0, EARLY)
        load_u(1)
        load_u(2)
        load_u(3)

        def gather(a, t, h):
            cols = slice(h * HALF, (h + 1) * HALF)
            nc.vector.tensor_tensor(
                picked[a][:, t, cols],
                x[a][t][:].indirect(offsets[:, h * HALF // 16 : (h + 1) * HALF // 16]),
                weights[:, cols],
                MULT,
            )

        def copy_on(engine):
            return nc.scalar.copy if engine == "S" else nc.vector.tensor_copy

        def group_x(a, c0, c1, engine):
            copy_on(engine)(
                out=x_grouped[a][:, c0:c1, :].rearrange("p (c i) t -> p c t i", i=4),
                in_=picked[a][:, :, c0:c1].rearrange("p t (c i) -> p c t i", i=4),
            )

        def quantize_x(a):
            nc.vector.quantize_mx(
                out=x_codes[:, a, :].bitcast(E4M3), scales=x_scales[:, a, :], in_=x_grouped[a][:].rearrange("p c t -> p (c t)")
            )

        def group_d(a, m0, m1, engine):
            copy_on(engine)(
                out=d_grouped[a][:].rearrange("p (t m j) -> p m t j", t=4, j=4)[:, m0:m1],
                in_=d_raw[a][:].rearrange("p j (m t) -> p m t j", t=4)[:, m0:m1],
            )

        def quantize_d(a):
            nc.vector.quantize_mx(out=d_codes[:, a, :].bitcast(E4M3), scales=d_scales[:, a, :], in_=d_grouped[a][:])

        def group_u(c, c0, c1, engine):
            copy_on(engine)(
                out=u_grouped[c][:, c0:c1, :].rearrange("p (c i) t -> p c t i", i=4),
                in_=u_raw[c][:, :, c0:c1].rearrange("p t (c i) -> p c t i", i=4),
            )

        def quantize_u(c):
            cols = slice(U_COLS * c, U_COLS * c + U_COLS)
            nc.vector.quantize_mx(
                out=u_codes[:, cols].bitcast(E4M3), scales=u_scales[:, cols], in_=u_grouped[c][:].rearrange("p c t -> p (c t)")
            )

        acc = {}

        def base(n, a):
            if a == 0:
                acc[n] = psum.tile([P, S], F32, name=f"acc{n}" if n < EARLY else f"bank{n - 4}")
            nc.tensor.matmul_mx(
                out=acc[n][:],
                lhsT=w_codes[:, a, 256 * n : 256 * n + 256].bitcast(E2M1),
                lhsT_scale=w_scales[:, a, 128 * n : 128 * n + 128],
                rhs=x_codes[:, a, :].bitcast(E4M3),
                rhs_scale=x_scales[:, a, :],
                start=(a == 0),
                stop=False,
            )

        h_bank = {}

        def low_rank(t, a):
            if a == 0:
                h_bank[t] = psum.tile([P, S], F32, name=f"bank{t}")
            nc.tensor.matmul_mx(
                out=h_bank[t][:],
                lhsT=d_codes[:, a, 128 * t : 128 * t + 128].bitcast(E4M3),
                lhsT_scale=d_scales[:, a, 128 * t : 128 * t + 128],
                rhs=x_codes[:, a, :].bitcast(E4M3),
                rhs_scale=x_scales[:, a, :],
                start=(a == 0),
                stop=(a == PASSES - 1),
            )

        def empty_h(t, engine):
            copy_on(engine)(out=h_flat[:, t, :], in_=h_bank[t][:])

        def group_h(c0, c1, engine):
            copy_on(engine)(
                out=h_grouped[:, c0:c1, :].rearrange("p (c i) t -> p c t i", i=4),
                in_=h_flat[:, :, c0:c1].rearrange("p t (c i) -> p c t i", i=4),
            )

        def quantize_h():
            nc.vector.quantize_mx(out=h_codes[:].bitcast(E4M3), scales=h_scales[:], in_=h_grouped[:].rearrange("p c t -> p (c t)"))

        def finish(n):
            nc.tensor.matmul_mx(
                out=acc[n][:],
                lhsT=u_codes[:, 128 * n : 128 * n + 128].bitcast(E4M3),
                lhsT_scale=u_scales[:, 128 * n : 128 * n + 128],
                rhs=h_codes[:].bitcast(E4M3),
                rhs_scale=h_scales[:],
                start=False,
                stop=True,
            )

        def empty_out(n, c0, c1, engine):
            copy_on(engine)(out=staged[n][:, c0:c1], in_=acc[n][:, c0:c1])

        def store(n):
            nc.sync.dma_start(out=out[128 * n : 128 * n + 128, :], in_=staged[n][:])

        gather(0, 0, 0)
        gather(0, 0, 1)
        gather(0, 1, 0)
        gather(0, 1, 1)
        gather(0, 2, 1)
        gather(0, 2, 0)
        gather(0, 3, 1)
        gather(0, 3, 0)
        group_x(0, HALF, S, "S")
        gather(1, 0, 0)
        gather(1, 0, 1)
        group_x(0, 0, HALF, "S")
        gather(1, 1, 0)
        gather(1, 2, 0)
        gather(1, 2, 1)
        gather(1, 3, 1)
        gather(1, 1, 1)
        gather(2, 0, 0)
        group_x(1, HALF, S, "S")
        gather(2, 0, 1)
        quantize_x(0)
        group_d(0, 0, 96, "S")
        group_d(0, 96, 128, "V")
        gather(1, 3, 0)
        gather(2, 1, 0)
        gather(2, 1, 1)
        group_x(1, 0, HALF, "S")
        gather(2, 2, 0)
        gather(2, 2, 1)
        quantize_x(1)
        quantize_d(0)
        group_d(1, 0, 96, "S")
        group_d(1, 96, 128, "V")
        low_rank(0, 0)
        low_rank(2, 0)
        gather(2, 3, 0)
        low_rank(1, 0)
        low_rank(3, 0)
        gather(2, 3, 1)
        group_x(2, 0, HALF, "S")
        quantize_d(1)
        group_x(2, HALF, S, "V")
        low_rank(1, 1)
        group_d(2, 0, 64, "S")
        low_rank(3, 1)
        group_d(2, 64, 128, "V")
        low_rank(0, 1)
        low_rank(2, 1)
        quantize_x(2)
        base(1, 0)
        base(2, 0)
        group_u(0, 0, 192, "S")
        base(3, 0)
        quantize_d(2)
        base(0, 0)
        base(2, 1)
        group_u(0, 192, 256, "V")
        base(1, 1)
        low_rank(1, 2)
        quantize_u(0)
        low_rank(3, 2)
        empty_h(1, "V")
        low_rank(2, 2)
        empty_h(3, "S")
        low_rank(0, 2)
        base(3, 1)
        empty_h(2, "V")
        base(0, 1)
        empty_h(0, "S")
        base(2, 2)
        group_u(1, 64, 256, "V")
        base(7, 0)
        base(6, 0)
        group_u(1, 0, 64, "S")
        base(7, 1)
        group_h(128, 512, "V")
        group_h(0, 128, "S")
        base(4, 0)
        base(0, 2)
        base(3, 2)
        quantize_u(1)
        base(1, 2)
        held = keep.tile([P, 2, U_COLS, 4], BF16, name="hflat", align_bytes=64)
        u_grouped[2] = held[:, 0]
        u_grouped[3] = held[:, 1]
        group_u(2, 0, 256, "S")
        quantize_h()
        base(5, 0)
        base(6, 1)
        base(5, 1)
        group_u(3, 0, 256, "V")
        finish(0)
        finish(1)
        empty_out(0, HALF, S, "V")
        empty_out(0, 0, HALF, "S")
        store(0)
        finish(3)
        base(5, 2)
        quantize_u(2)
        empty_out(1, 0, S, "S")
        store(1)
        finish(2)
        empty_out(3, 0, S, "V")
        store(3)
        base(6, 2)
        finish(5)
        empty_out(2, 0, S, "S")
        store(2)
        quantize_u(3)
        base(7, 2)
        base(4, 1)
        empty_out(5, 0, S, "V")
        store(5)
        finish(7)
        finish(6)
        empty_out(7, 0, S, "V")
        store(7)
        base(4, 2)
        empty_out(6, 0, S, "S")
        store(6)
        finish(4)
        empty_out(4, 0, S, "V")
        store(4)
